import numpy as np
import ml_dtypes

BF16 = ml_dtypes.bfloat16


def bf(x):
    return np.asarray(x, np.float32).astype(BF16)


def f32(x):
    return np.asarray(x, np.float32)


def f64(x):
    return np.asarray(x).astype(np.float64)


def striped(idx):
    return np.tile(idx.reshape(-1, 16).T, (8, 1))


S, K, M, N, E, Q = 256, 128, 512, 192, 2, 96


def setup_inputs():
    return {"base": bf(np.random.standard_normal((M, S))), "x": bf(np.random.standard_normal((K, N))), "w": bf(np.random.standard_normal((E, K, M)) / np.sqrt(K)), "s": f32(0.5 + np.random.random_sample((M, 1))), "b": f32(0.5 * np.random.standard_normal((M, 1))), "offs": striped(np.random.permutation(S)[:N])}


def reference(base, x, w, s, b, offs):
    idx = offs[:16].T.reshape(-1)
    z = f64(base).copy()
    for e in range(E):
        z[:, idx[e * Q : (e + 1) * Q]] += f64(w)[e].T @ f64(x)[:, e * Q : (e + 1) * Q]
    return z * f64(s) + f64(b)

@@ -1,0 +1,76 @@
+import concourse.mybir as mybir
+from concourse.masks import make_identity
+
+BF16 = mybir.dt.bfloat16
+F32 = mybir.dt.float32
+U16 = mybir.dt.uint16
+
+P = 128
+TOKENS = 256
+FEATURES = 512
+ENTRIES = 192
+EXPERTS = 2
+PIECE = ENTRIES // EXPERTS
+PIECE_COLUMNS = PIECE // 16
+BLOCKS = FEATURES // P
+
+FLOPS = 2 * P * FEATURES * ENTRIES
+
+
+def tile_scatter_matmul_kernel(tc, base, x, w, s, b, offs, out):
+    nc = tc.nc
+    mult, add = mybir.AluOpType.mult, mybir.AluOpType.add
+    identity_func = mybir.ActivationFunctionType.Identity
+
+    with (
+        tc.tile_pool(name="held", bufs=1) as held,
+        tc.psum_pool(name="banks", bufs=1) as banks,
+    ):
+        offsets = held.tile([P, ENTRIES // 16], U16, name="offsets")
+        nc.sync.dma_start(offsets[:], offs)
+
+        base_rows = held.tile([P, BLOCKS, TOKENS], BF16, name="base_rows")
+        nc.scalar.dma_start(base_rows[:], base.rearrange("(a p) t -> p a t", p=P))
+
+        tokens_in = held.tile([P, ENTRIES], BF16, name="tokens_in")
+        nc.sync.dma_start(tokens_in[:], x)
+
+        weights = held.tile([P, EXPERTS, FEATURES], BF16, name="weights")
+        nc.sync.dma_start(weights[:], w.rearrange("e k m -> k e m"))
+
+        ident = held.tile([P, P], BF16, name="ident")
+        make_identity(nc, ident[:])
+
+        gain = held.tile([P, BLOCKS], F32, name="gain")
+        shift = held.tile([P, BLOCKS], F32, name="shift")
+        with nc.allow_non_contiguous_dma(reason="one float32 to a partition for each block"):
+            nc.gpsimd.dma_start(gain[:], s.rearrange("(a p) o -> p (a o)", p=P))
+            nc.gpsimd.dma_start(shift[:], b.rearrange("(a p) o -> p (a o)", p=P))
+
+        windows = [banks.tile([P, TOKENS], F32, name=f"window{a}") for a in range(BLOCKS)]
+        for a in range(BLOCKS):
+            nc.tensor.matmul(windows[a][:], ident[:], base_rows[:, a, :], start=True, stop=False)
+
+        for a in range(BLOCKS):
+            for e in range(EXPERTS):
+                nc.tensor.matmul(
+                    windows[a][:].indirect(offsets[:, e * PIECE_COLUMNS : (e + 1) * PIECE_COLUMNS]),
+                    weights[:, e, a * P : (a + 1) * P],
+                    tokens_in[:, e * PIECE : (e + 1) * PIECE],
+                    start=False,
+                    stop=(e == EXPERTS - 1),
+                )
+
+        out_blocks = out.rearrange("(a p) t -> a p t", p=P)
+        for a in range(BLOCKS):
+            result = held.tile([P, TOKENS], F32, name=f"result{a}")
+            if a % 2 == 0:
+                nc.vector.tensor_scalar(
+                    result[:], windows[a][:], gain[:, a : a + 1], shift[:, a : a + 1], op0=mult, op1=add
+                )
+                nc.sync.dma_start(out_blocks[a], result[:])
+            else:
+                nc.scalar.activation(
+                    result[:], windows[a][:], identity_func, bias=shift[:, a : a + 1], scale=gain[:, a : a + 1]
+                )
+                nc.scalar.dma_start(out_blocks[a], result[:])

@@ -14,23 +14,33 @@ PIECE = ENTRIES // EXPERTS
 PIECE_COLUMNS = PIECE // 16
 BLOCKS = FEATURES // P
 
+WARM_COLUMNS = 512
+WARM_MATMULS = 3
+
 FLOPS = 2 * P * FEATURES * ENTRIES
 
 
 def tile_scatter_matmul_kernel(tc, base, x, w, s, b, offs, out):
     nc = tc.nc
     mult, add = mybir.AluOpType.mult, mybir.AluOpType.add
-    identity_func = mybir.ActivationFunctionType.Identity
 
     with (
         tc.tile_pool(name="held", bufs=1) as held,
         tc.psum_pool(name="banks", bufs=1) as banks,
     ):
+        zeros = held.tile([P, WARM_COLUMNS], BF16, name="zeros")
+        nc.gpsimd.memset(zeros[:], 0.0)
+        spare = banks.tile([P, WARM_COLUMNS], F32, name="spare")
+        for i in range(WARM_MATMULS):
+            nc.tensor.matmul(spare[:], zeros[:, 0:P], zeros[:], start=True, stop=True)
+
         offsets = held.tile([P, ENTRIES // 16], U16, name="offsets")
         nc.sync.dma_start(offsets[:], offs)
 
+        base_blocks = base.rearrange("(a p) t -> p a t", p=P)
         base_rows = held.tile([P, BLOCKS, TOKENS], BF16, name="base_rows")
-        nc.scalar.dma_start(base_rows[:], base.rearrange("(a p) t -> p a t", p=P))
+        for a in range(0, BLOCKS, 2):
+            nc.scalar.dma_start(base_rows[:, a : a + 2, :], base_blocks[:, a : a + 2, :])
 
         tokens_in = held.tile([P, ENTRIES], BF16, name="tokens_in")
         nc.sync.dma_start(tokens_in[:], x)
@@ -38,14 +48,14 @@ def tile_scatter_matmul_kernel(tc, base, x, w, s, b, offs, out):
         weights = held.tile([P, EXPERTS, FEATURES], BF16, name="weights")
         nc.sync.dma_start(weights[:], w.rearrange("e k m -> k e m"))
 
-        ident = held.tile([P, P], BF16, name="ident")
-        make_identity(nc, ident[:])
-
         gain = held.tile([P, BLOCKS], F32, name="gain")
         shift = held.tile([P, BLOCKS], F32, name="shift")
         with nc.allow_non_contiguous_dma(reason="one float32 to a partition for each block"):
-            nc.gpsimd.dma_start(gain[:], s.rearrange("(a p) o -> p (a o)", p=P))
-            nc.gpsimd.dma_start(shift[:], b.rearrange("(a p) o -> p (a o)", p=P))
+            nc.sync.dma_start(gain[:], s.rearrange("(a p) o -> p (a o)", p=P))
+            nc.scalar.dma_start(shift[:], b.rearrange("(a p) o -> p (a o)", p=P))
+
+        ident = held.tile([P, P], BF16, name="ident")
+        make_identity(nc, ident[:])
 
         windows = [banks.tile([P, TOKENS], F32, name=f"window{a}") for a in range(BLOCKS)]
         for a in range(BLOCKS):
@@ -64,13 +74,8 @@ def tile_scatter_matmul_kernel(tc, base, x, w, s, b, offs, out):
         out_blocks = out.rearrange("(a p) t -> a p t", p=P)
         for a in range(BLOCKS):
             result = held.tile([P, TOKENS], F32, name=f"result{a}")
-            if a % 2 == 0:
-                nc.vector.tensor_scalar(
-                    result[:], windows[a][:], gain[:, a : a + 1], shift[:, a : a + 1], op0=mult, op1=add
-                )
-                nc.sync.dma_start(out_blocks[a], result[:])
-            else:
-                nc.scalar.activation(
-                    result[:], windows[a][:], identity_func, bias=shift[:, a : a + 1], scale=gain[:, a : a + 1]
-                )
-                nc.scalar.dma_start(out_blocks[a], result[:])
+            nc.vector.tensor_scalar(
+                result[:], windows[a][:], gain[:, a : a + 1], shift[:, a : a + 1], op0=mult, op1=add
+            )
+            store_queue = nc.sync if a % 2 == 0 else nc.scalar
+            store_queue.dma_start(out_blocks[a], result[:])

@@ -48,18 +48,24 @@ def tile_scatter_matmul_kernel(tc, base, x, w, s, b, offs, out):
         weights = held.tile([P, EXPERTS, FEATURES], BF16, name="weights")
         nc.sync.dma_start(weights[:], w.rearrange("e k m -> k e m"))
 
-        gain = held.tile([P, BLOCKS], F32, name="gain")
-        shift = held.tile([P, BLOCKS], F32, name="shift")
-        with nc.allow_non_contiguous_dma(reason="one float32 to a partition for each block"):
-            nc.sync.dma_start(gain[:], s.rearrange("(a p) o -> p (a o)", p=P))
-            nc.scalar.dma_start(shift[:], b.rearrange("(a p) o -> p (a o)", p=P))
+        affine_rows = held.tile([P, P], F32, name="affine_rows")
+        nc.vector.memset(affine_rows[:], 0.0)
+        nc.sync.dma_start(affine_rows[0:BLOCKS, :], s.rearrange("(a p) o -> a (p o)", p=P))
+        nc.scalar.dma_start(affine_rows[BLOCKS : 2 * BLOCKS, :], b.rearrange("(a p) o -> a (p o)", p=P))
 
         ident = held.tile([P, P], BF16, name="ident")
         make_identity(nc, ident[:])
+        ident_f32 = held.tile([P, P], F32, name="ident_f32")
+        nc.vector.tensor_copy(ident_f32[:], ident[:])
 
         windows = [banks.tile([P, TOKENS], F32, name=f"window{a}") for a in range(BLOCKS)]
         for a in range(BLOCKS):
             nc.tensor.matmul(windows[a][:], ident[:], base_rows[:, a, :], start=True, stop=False)
+
+        affine_bank = banks.tile([P, P], F32, name="affine_bank")
+        nc.tensor.transpose(affine_bank[:], affine_rows[:], ident_f32[:])
+        affine = held.tile([P, 2 * BLOCKS], F32, name="affine")
+        nc.vector.tensor_copy(affine[:], affine_bank[:, 0 : 2 * BLOCKS])
 
         for a in range(BLOCKS):
             for e in range(EXPERTS):
@@ -75,7 +81,12 @@ def tile_scatter_matmul_kernel(tc, base, x, w, s, b, offs, out):
         for a in range(BLOCKS):
             result = held.tile([P, TOKENS], F32, name=f"result{a}")
             nc.vector.tensor_scalar(
-                result[:], windows[a][:], gain[:, a : a + 1], shift[:, a : a + 1], op0=mult, op1=add
+                result[:],
+                windows[a][:],
+                affine[:, a : a + 1],
+                affine[:, BLOCKS + a : BLOCKS + a + 1],
+                op0=mult,
+                op1=add,
             )
             store_queue = nc.sync if a % 2 == 0 else nc.scalar
             store_queue.dma_start(out_blocks[a], result[:])

@@ -14,9 +14,6 @@ PIECE = ENTRIES // EXPERTS
 PIECE_COLUMNS = PIECE // 16
 BLOCKS = FEATURES // P
 
-WARM_COLUMNS = 512
-WARM_MATMULS = 3
-
 FLOPS = 2 * P * FEATURES * ENTRIES
 
 
@@ -28,12 +25,6 @@ def tile_scatter_matmul_kernel(tc, base, x, w, s, b, offs, out):
         tc.tile_pool(name="held", bufs=1) as held,
         tc.psum_pool(name="banks", bufs=1) as banks,
     ):
-        zeros = held.tile([P, WARM_COLUMNS], BF16, name="zeros")
-        nc.gpsimd.memset(zeros[:], 0.0)
-        spare = banks.tile([P, WARM_COLUMNS], F32, name="spare")
-        for i in range(WARM_MATMULS):
-            nc.tensor.matmul(spare[:], zeros[:, 0:P], zeros[:], start=True, stop=True)
-
         offsets = held.tile([P, ENTRIES // 16], U16, name="offsets")
         nc.sync.dma_start(offsets[:], offs)
 
@@ -48,24 +39,18 @@ def tile_scatter_matmul_kernel(tc, base, x, w, s, b, offs, out):
         weights = held.tile([P, EXPERTS, FEATURES], BF16, name="weights")
         nc.sync.dma_start(weights[:], w.rearrange("e k m -> k e m"))
 
-        affine_rows = held.tile([P, P], F32, name="affine_rows")
-        nc.vector.memset(affine_rows[:], 0.0)
-        nc.sync.dma_start(affine_rows[0:BLOCKS, :], s.rearrange("(a p) o -> a (p o)", p=P))
-        nc.scalar.dma_start(affine_rows[BLOCKS : 2 * BLOCKS, :], b.rearrange("(a p) o -> a (p o)", p=P))
+        gain = held.tile([P, BLOCKS], F32, name="gain")
+        shift = held.tile([P, BLOCKS], F32, name="shift")
+        with nc.allow_non_contiguous_dma(reason="one float32 to a partition for each block"):
+            nc.sync.dma_start(gain[:], s.rearrange("(a p) o -> p (a o)", p=P))
+            nc.scalar.dma_start(shift[:], b.rearrange("(a p) o -> p (a o)", p=P))
 
         ident = held.tile([P, P], BF16, name="ident")
         make_identity(nc, ident[:])
-        ident_f32 = held.tile([P, P], F32, name="ident_f32")
-        nc.vector.tensor_copy(ident_f32[:], ident[:])
 
         windows = [banks.tile([P, TOKENS], F32, name=f"window{a}") for a in range(BLOCKS)]
         for a in range(BLOCKS):
             nc.tensor.matmul(windows[a][:], ident[:], base_rows[:, a, :], start=True, stop=False)
-
-        affine_bank = banks.tile([P, P], F32, name="affine_bank")
-        nc.tensor.transpose(affine_bank[:], affine_rows[:], ident_f32[:])
-        affine = held.tile([P, 2 * BLOCKS], F32, name="affine")
-        nc.vector.tensor_copy(affine[:], affine_bank[:, 0 : 2 * BLOCKS])
 
         for a in range(BLOCKS):
             for e in range(EXPERTS):
@@ -81,12 +66,7 @@ def tile_scatter_matmul_kernel(tc, base, x, w, s, b, offs, out):
         for a in range(BLOCKS):
             result = held.tile([P, TOKENS], F32, name=f"result{a}")
             nc.vector.tensor_scalar(
-                result[:],
-                windows[a][:],
-                affine[:, a : a + 1],
-                affine[:, BLOCKS + a : BLOCKS + a + 1],
-                op0=mult,
-                op1=add,
+                result[:], windows[a][:], gain[:, a : a + 1], shift[:, a : a + 1], op0=mult, op1=add
             )
             store_queue = nc.sync if a % 2 == 0 else nc.scalar
             store_queue.dma_start(out_blocks[a], result[:])

@@ -25,24 +25,28 @@ def tile_scatter_matmul_kernel(tc, base, x, w, s, b, offs, out):
         tc.tile_pool(name="held", bufs=1) as held,
         tc.psum_pool(name="banks", bufs=1) as banks,
     ):
-        offsets = held.tile([P, ENTRIES // 16], U16, name="offsets")
-        nc.sync.dma_start(offsets[:], offs)
+        HALF = BLOCKS // 2
 
         base_blocks = base.rearrange("(a p) t -> p a t", p=P)
         base_rows = held.tile([P, BLOCKS, TOKENS], BF16, name="base_rows")
-        for a in range(0, BLOCKS, 2):
-            nc.scalar.dma_start(base_rows[:, a : a + 2, :], base_blocks[:, a : a + 2, :])
+        nc.sync.dma_start(base_rows[:, 0:HALF, :], base_blocks[:, 0:HALF, :])
+        nc.scalar.dma_start(base_rows[:, HALF:BLOCKS, :], base_blocks[:, HALF:BLOCKS, :])
+
+        offsets = held.tile([P, ENTRIES // 16], U16, name="offsets")
+        nc.sync.dma_start(offsets[:], offs)
 
         tokens_in = held.tile([P, ENTRIES], BF16, name="tokens_in")
-        nc.sync.dma_start(tokens_in[:], x)
+        nc.scalar.dma_start(tokens_in[:], x)
 
+        w_by_k = w.rearrange("e k m -> k e m")
         weights = held.tile([P, EXPERTS, FEATURES], BF16, name="weights")
-        nc.sync.dma_start(weights[:], w.rearrange("e k m -> k e m"))
+        nc.sync.dma_start(weights[:, :, 0 : HALF * P], w_by_k[:, :, 0 : HALF * P])
+        nc.sync.dma_start(weights[:, :, HALF * P : FEATURES], w_by_k[:, :, HALF * P : FEATURES])
 
         gain = held.tile([P, BLOCKS], F32, name="gain")
         shift = held.tile([P, BLOCKS], F32, name="shift")
         with nc.allow_non_contiguous_dma(reason="one float32 to a partition for each block"):
-            nc.sync.dma_start(gain[:], s.rearrange("(a p) o -> p (a o)", p=P))
+            nc.scalar.dma_start(gain[:], s.rearrange("(a p) o -> p (a o)", p=P))
             nc.scalar.dma_start(shift[:], b.rearrange("(a p) o -> p (a o)", p=P))
 
         ident = held.tile([P, P], BF16, name="ident")

@@ -30,13 +30,13 @@ def tile_scatter_matmul_kernel(tc, base, x, w, s, b, offs, out):
         base_blocks = base.rearrange("(a p) t -> p a t", p=P)
         base_rows = held.tile([P, BLOCKS, TOKENS], BF16, name="base_rows")
         nc.sync.dma_start(base_rows[:, 0:HALF, :], base_blocks[:, 0:HALF, :])
-        nc.scalar.dma_start(base_rows[:, HALF:BLOCKS, :], base_blocks[:, HALF:BLOCKS, :])
+        nc.sync.dma_start(base_rows[:, HALF:BLOCKS, :], base_blocks[:, HALF:BLOCKS, :])
 
         offsets = held.tile([P, ENTRIES // 16], U16, name="offsets")
         nc.sync.dma_start(offsets[:], offs)
 
         tokens_in = held.tile([P, ENTRIES], BF16, name="tokens_in")
-        nc.scalar.dma_start(tokens_in[:], x)
+        nc.sync.dma_start(tokens_in[:], x)
 
         w_by_k = w.rearrange("e k m -> k e m")
         weights = held.tile([P, EXPERTS, FEATURES], BF16, name="weights")
@@ -46,8 +46,8 @@ def tile_scatter_matmul_kernel(tc, base, x, w, s, b, offs, out):
         gain = held.tile([P, BLOCKS], F32, name="gain")
         shift = held.tile([P, BLOCKS], F32, name="shift")
         with nc.allow_non_contiguous_dma(reason="one float32 to a partition for each block"):
-            nc.scalar.dma_start(gain[:], s.rearrange("(a p) o -> p (a o)", p=P))
-            nc.scalar.dma_start(shift[:], b.rearrange("(a p) o -> p (a o)", p=P))
+            nc.sync.dma_start(gain[:], s.rearrange("(a p) o -> p (a o)", p=P))
+            nc.sync.dma_start(shift[:], b.rearrange("(a p) o -> p (a o)", p=P))
 
         ident = held.tile([P, P], BF16, name="ident")
         make_identity(nc, ident[:])

@@ -25,6 +25,10 @@ def tile_scatter_matmul_kernel(tc, base, x, w, s, b, offs, out):
         tc.tile_pool(name="held", bufs=1) as held,
         tc.psum_pool(name="banks", bufs=1) as banks,
     ):
+        gain_shift_rows = held.tile([2 * BLOCKS, P], F32, name="gain_shift_rows")
+        nc.scalar.dma_start(gain_shift_rows[0:BLOCKS, :], s.rearrange("(a p) o -> a (p o)", p=P))
+        nc.scalar.dma_start(gain_shift_rows[BLOCKS : 2 * BLOCKS, :], b.rearrange("(a p) o -> a (p o)", p=P))
+
         HALF = BLOCKS // 2
 
         base_blocks = base.rearrange("(a p) t -> p a t", p=P)
@@ -43,14 +47,15 @@ def tile_scatter_matmul_kernel(tc, base, x, w, s, b, offs, out):
         nc.sync.dma_start(weights[:, :, 0 : HALF * P], w_by_k[:, :, 0 : HALF * P])
         nc.sync.dma_start(weights[:, :, HALF * P : FEATURES], w_by_k[:, :, HALF * P : FEATURES])
 
-        gain = held.tile([P, BLOCKS], F32, name="gain")
-        shift = held.tile([P, BLOCKS], F32, name="shift")
-        with nc.allow_non_contiguous_dma(reason="one float32 to a partition for each block"):
-            nc.sync.dma_start(gain[:], s.rearrange("(a p) o -> p (a o)", p=P))
-            nc.sync.dma_start(shift[:], b.rearrange("(a p) o -> p (a o)", p=P))
-
         ident = held.tile([P, P], BF16, name="ident")
         make_identity(nc, ident[:])
+
+        small_ident = held.tile([2 * BLOCKS, 2 * BLOCKS], F32, name="small_ident")
+        nc.vector.tensor_copy(small_ident[:], ident[0 : 2 * BLOCKS, 0 : 2 * BLOCKS])
+        gain_shift_bank = banks.tile([P, 2 * BLOCKS], F32, name="gain_shift_bank")
+        nc.tensor.matmul(gain_shift_bank[:], gain_shift_rows[:], small_ident[:], start=True, stop=True)
+        gain_shift = held.tile([P, 2 * BLOCKS], F32, name="gain_shift")
+        nc.vector.tensor_copy(gain_shift[:], gain_shift_bank[:])
 
         windows = [banks.tile([P, TOKENS], F32, name=f"window{a}") for a in range(BLOCKS)]
         for a in range(BLOCKS):
@@ -70,7 +75,12 @@ def tile_scatter_matmul_kernel(tc, base, x, w, s, b, offs, out):
         for a in range(BLOCKS):
             result = held.tile([P, TOKENS], F32, name=f"result{a}")
             nc.vector.tensor_scalar(
-                result[:], windows[a][:], gain[:, a : a + 1], shift[:, a : a + 1], op0=mult, op1=add
+                result[:],
+                windows[a][:],
+                gain_shift[:, a : a + 1],
+                gain_shift[:, BLOCKS + a : BLOCKS + a + 1],
+                op0=mult,
+                op1=add,
             )
             store_queue = nc.sync if a % 2 == 0 else nc.scalar
             store_queue.dma_start(out_blocks[a], result[:])

@@ -14,6 +14,9 @@ PIECE = ENTRIES // EXPERTS
 PIECE_COLUMNS = PIECE // 16
 BLOCKS = FEATURES // P
 
+WARM_COLUMNS = 512
+WARM_MATMULS = 4
+
 FLOPS = 2 * P * FEATURES * ENTRIES
 
 
@@ -25,6 +28,12 @@ def tile_scatter_matmul_kernel(tc, base, x, w, s, b, offs, out):
         tc.tile_pool(name="held", bufs=1) as held,
         tc.psum_pool(name="banks", bufs=1) as banks,
     ):
+        zeros = held.tile([P, WARM_COLUMNS], BF16, name="zeros")
+        nc.vector.memset(zeros[:], 0.0)
+        spare_bank = banks.tile([P, WARM_COLUMNS], F32, name="spare_bank")
+        for i in range(WARM_MATMULS):
+            nc.tensor.matmul(spare_bank[:], zeros[:, 0:P], zeros[:], start=True, stop=True)
+
         gain_shift_rows = held.tile([2 * BLOCKS, P], F32, name="gain_shift_rows")
         nc.scalar.dma_start(gain_shift_rows[0:BLOCKS, :], s.rearrange("(a p) o -> a (p o)", p=P))
         nc.scalar.dma_start(gain_shift_rows[BLOCKS : 2 * BLOCKS, :], b.rearrange("(a p) o -> a (p o)", p=P))
@@ -50,16 +59,16 @@ def tile_scatter_matmul_kernel(tc, base, x, w, s, b, offs, out):
         ident = held.tile([P, P], BF16, name="ident")
         make_identity(nc, ident[:])
 
+        windows = [banks.tile([P, TOKENS], F32, name=f"window{a}") for a in range(BLOCKS)]
+        for a in range(BLOCKS):
+            nc.tensor.matmul(windows[a][:], ident[:], base_rows[:, a, :], start=True, stop=False)
+
         small_ident = held.tile([2 * BLOCKS, 2 * BLOCKS], F32, name="small_ident")
         nc.vector.tensor_copy(small_ident[:], ident[0 : 2 * BLOCKS, 0 : 2 * BLOCKS])
         gain_shift_bank = banks.tile([P, 2 * BLOCKS], F32, name="gain_shift_bank")
         nc.tensor.matmul(gain_shift_bank[:], gain_shift_rows[:], small_ident[:], start=True, stop=True)
         gain_shift = held.tile([P, 2 * BLOCKS], F32, name="gain_shift")
         nc.vector.tensor_copy(gain_shift[:], gain_shift_bank[:])
-
-        windows = [banks.tile([P, TOKENS], F32, name=f"window{a}") for a in range(BLOCKS)]
-        for a in range(BLOCKS):
-            nc.tensor.matmul(windows[a][:], ident[:], base_rows[:, a, :], start=True, stop=False)
 
         for a in range(BLOCKS):
             for e in range(EXPERTS):

@@ -15,7 +15,7 @@ PIECE_COLUMNS = PIECE // 16
 BLOCKS = FEATURES // P
 
 WARM_COLUMNS = 512
-WARM_MATMULS = 4
+WARM_MATMULS = 2
 
 FLOPS = 2 * P * FEATURES * ENTRIES
 

@@ -34,7 +34,8 @@ def tile_scatter_matmul_kernel(tc, base, x, w, s, b, offs, out):
         for i in range(WARM_MATMULS):
             nc.tensor.matmul(spare_bank[:], zeros[:, 0:P], zeros[:], start=True, stop=True)
 
-        gain_shift_rows = held.tile([2 * BLOCKS, P], F32, name="gain_shift_rows")
+        gain_shift_rows = held.tile([P, P], F32, name="gain_shift_rows")
+        nc.vector.memset(gain_shift_rows[:], 0.0)
         nc.scalar.dma_start(gain_shift_rows[0:BLOCKS, :], s.rearrange("(a p) o -> a (p o)", p=P))
         nc.scalar.dma_start(gain_shift_rows[BLOCKS : 2 * BLOCKS, :], b.rearrange("(a p) o -> a (p o)", p=P))
 
@@ -63,12 +64,12 @@ def tile_scatter_matmul_kernel(tc, base, x, w, s, b, offs, out):
         for a in range(BLOCKS):
             nc.tensor.matmul(windows[a][:], ident[:], base_rows[:, a, :], start=True, stop=False)
 
-        small_ident = held.tile([2 * BLOCKS, 2 * BLOCKS], F32, name="small_ident")
-        nc.vector.tensor_copy(small_ident[:], ident[0 : 2 * BLOCKS, 0 : 2 * BLOCKS])
-        gain_shift_bank = banks.tile([P, 2 * BLOCKS], F32, name="gain_shift_bank")
-        nc.tensor.matmul(gain_shift_bank[:], gain_shift_rows[:], small_ident[:], start=True, stop=True)
+        ident_f32 = held.tile([P, P], F32, name="ident_f32")
+        nc.vector.tensor_copy(ident_f32[:], ident[:])
+        gain_shift_bank = banks.tile([P, P], F32, name="gain_shift_bank")
+        nc.tensor.transpose(gain_shift_bank[:], gain_shift_rows[:], ident_f32[:])
         gain_shift = held.tile([P, 2 * BLOCKS], F32, name="gain_shift")
-        nc.vector.tensor_copy(gain_shift[:], gain_shift_bank[:])
+        nc.vector.tensor_copy(gain_shift[:], gain_shift_bank[:, 0 : 2 * BLOCKS])
 
         for a in range(BLOCKS):
             for e in range(EXPERTS):

@@ -34,17 +34,17 @@ def tile_scatter_matmul_kernel(tc, base, x, w, s, b, offs, out):
         for i in range(WARM_MATMULS):
             nc.tensor.matmul(spare_bank[:], zeros[:, 0:P], zeros[:], start=True, stop=True)
 
-        gain_shift_rows = held.tile([P, P], F32, name="gain_shift_rows")
-        nc.vector.memset(gain_shift_rows[:], 0.0)
-        nc.scalar.dma_start(gain_shift_rows[0:BLOCKS, :], s.rearrange("(a p) o -> a (p o)", p=P))
-        nc.scalar.dma_start(gain_shift_rows[BLOCKS : 2 * BLOCKS, :], b.rearrange("(a p) o -> a (p o)", p=P))
-
         HALF = BLOCKS // 2
 
         base_blocks = base.rearrange("(a p) t -> p a t", p=P)
         base_rows = held.tile([P, BLOCKS, TOKENS], BF16, name="base_rows")
         nc.sync.dma_start(base_rows[:, 0:HALF, :], base_blocks[:, 0:HALF, :])
         nc.sync.dma_start(base_rows[:, HALF:BLOCKS, :], base_blocks[:, HALF:BLOCKS, :])
+
+        gain_shift_rows = held.tile([P, P], F32, name="gain_shift_rows")
+        nc.vector.memset(gain_shift_rows[:], 0.0)
+        nc.sync.dma_start(gain_shift_rows[0:BLOCKS, :], s.rearrange("(a p) o -> a (p o)", p=P))
+        nc.sync.dma_start(gain_shift_rows[BLOCKS : 2 * BLOCKS, :], b.rearrange("(a p) o -> a (p o)", p=P))
 
         offsets = held.tile([P, ENTRIES // 16], U16, name="offsets")
         nc.sync.dma_start(offsets[:], offs)

@@ -92,5 +92,4 @@ def tile_scatter_matmul_kernel(tc, base, x, w, s, b, offs, out):
                 op0=mult,
                 op1=add,
             )
-            store_queue = nc.sync if a % 2 == 0 else nc.scalar
-            store_queue.dma_start(out_blocks[a], result[:])
+            nc.sync.dma_start(out_blocks[a], result[:])

@@ -42,7 +42,7 @@ def tile_scatter_matmul_kernel(tc, base, x, w, s, b, offs, out):
         nc.sync.dma_start(base_rows[:, HALF:BLOCKS, :], base_blocks[:, HALF:BLOCKS, :])
 
         gain_shift_rows = held.tile([P, P], F32, name="gain_shift_rows")
-        nc.vector.memset(gain_shift_rows[:], 0.0)
+        nc.gpsimd.memset(gain_shift_rows[:], 0.0)
         nc.sync.dma_start(gain_shift_rows[0:BLOCKS, :], s.rearrange("(a p) o -> a (p o)", p=P))
         nc.sync.dma_start(gain_shift_rows[BLOCKS : 2 * BLOCKS, :], b.rearrange("(a p) o -> a (p o)", p=P))
 

@@ -66,10 +66,8 @@ def tile_scatter_matmul_kernel(tc, base, x, w, s, b, offs, out):
 
         ident_f32 = held.tile([P, P], F32, name="ident_f32")
         nc.vector.tensor_copy(ident_f32[:], ident[:])
-        gain_shift_bank = banks.tile([P, P], F32, name="gain_shift_bank")
-        nc.tensor.transpose(gain_shift_bank[:], gain_shift_rows[:], ident_f32[:])
-        gain_shift = held.tile([P, 2 * BLOCKS], F32, name="gain_shift")
-        nc.vector.tensor_copy(gain_shift[:], gain_shift_bank[:, 0 : 2 * BLOCKS])
+        gain_shift = banks.tile([P, P], F32, name="gain_shift")
+        nc.tensor.transpose(gain_shift[:], gain_shift_rows[:], ident_f32[:])
 
         for a in range(BLOCKS):
             for e in range(EXPERTS):

@@ -36,6 +36,9 @@ def tile_scatter_matmul_kernel(tc, base, x, w, s, b, offs, out):
 
         HALF = BLOCKS // 2
 
+        offsets = held.tile([P, ENTRIES // 16], U16, name="offsets")
+        nc.sync.dma_start(offsets[:], offs)
+
         base_blocks = base.rearrange("(a p) t -> p a t", p=P)
         base_rows = held.tile([P, BLOCKS, TOKENS], BF16, name="base_rows")
         nc.sync.dma_start(base_rows[:, 0:HALF, :], base_blocks[:, 0:HALF, :])
@@ -46,16 +49,14 @@ def tile_scatter_matmul_kernel(tc, base, x, w, s, b, offs, out):
         nc.sync.dma_start(gain_shift_rows[0:BLOCKS, :], s.rearrange("(a p) o -> a (p o)", p=P))
         nc.sync.dma_start(gain_shift_rows[BLOCKS : 2 * BLOCKS, :], b.rearrange("(a p) o -> a (p o)", p=P))
 
-        offsets = held.tile([P, ENTRIES // 16], U16, name="offsets")
-        nc.sync.dma_start(offsets[:], offs)
-
         tokens_in = held.tile([P, ENTRIES], BF16, name="tokens_in")
         nc.sync.dma_start(tokens_in[:], x)
 
         w_by_k = w.rearrange("e k m -> k e m")
         weights = held.tile([P, EXPERTS, FEATURES], BF16, name="weights")
-        nc.sync.dma_start(weights[:, :, 0 : HALF * P], w_by_k[:, :, 0 : HALF * P])
-        nc.sync.dma_start(weights[:, :, HALF * P : FEATURES], w_by_k[:, :, HALF * P : FEATURES])
+        for first_block, end_block in ((0, 1), (1, 2), (2, BLOCKS)):
+            columns = slice(first_block * P, end_block * P)
+            nc.sync.dma_start(weights[:, :, columns], w_by_k[:, :, columns])
 
         ident = held.tile([P, P], BF16, name="ident")
         make_identity(nc, ident[:])

@@ -23,6 +23,7 @@ FLOPS = 2 * P * FEATURES * ENTRIES
 def tile_scatter_matmul_kernel(tc, base, x, w, s, b, offs, out):
     nc = tc.nc
     mult, add = mybir.AluOpType.mult, mybir.AluOpType.add
+    identity_function = mybir.ActivationFunctionType.Identity
 
     with (
         tc.tile_pool(name="held", bufs=1) as held,
@@ -33,6 +34,9 @@ def tile_scatter_matmul_kernel(tc, base, x, w, s, b, offs, out):
         spare_bank = banks.tile([P, WARM_COLUMNS], F32, name="spare_bank")
         for i in range(WARM_MATMULS):
             nc.tensor.matmul(spare_bank[:], zeros[:, 0:P], zeros[:], start=True, stop=True)
+
+        table_warmer = held.tile([P, 1], F32, name="table_warmer")
+        nc.scalar.activation(table_warmer[:], zeros[:, 0:1], identity_function)
 
         HALF = BLOCKS // 2
 
@@ -54,9 +58,12 @@ def tile_scatter_matmul_kernel(tc, base, x, w, s, b, offs, out):
 
         w_by_k = w.rearrange("e k m -> k e m")
         weights = held.tile([P, EXPERTS, FEATURES], BF16, name="weights")
-        for first_block, end_block in ((0, 1), (1, 2), (2, BLOCKS)):
-            columns = slice(first_block * P, end_block * P)
+        for a in range(HALF):
+            columns = slice(a * P, (a + 1) * P)
             nc.sync.dma_start(weights[:, :, columns], w_by_k[:, :, columns])
+        last_columns = slice(HALF * P, BLOCKS * P)
+        for e in range(EXPERTS):
+            nc.sync.dma_start(weights[:, e, last_columns], w_by_k[:, e, last_columns])
 
         ident = held.tile([P, P], BF16, name="ident")
         make_identity(nc, ident[:])
@@ -69,26 +76,44 @@ def tile_scatter_matmul_kernel(tc, base, x, w, s, b, offs, out):
         nc.vector.tensor_copy(ident_f32[:], ident[:])
         gain_shift = banks.tile([P, P], F32, name="gain_shift")
         nc.tensor.transpose(gain_shift[:], gain_shift_rows[:], ident_f32[:])
+        gain_shift_copy = held.tile([P, 2 * BLOCKS], F32, name="gain_shift_copy")
+        nc.vector.tensor_copy(gain_shift_copy[:], gain_shift[:, 0 : 2 * BLOCKS])
 
-        for a in range(BLOCKS):
-            for e in range(EXPERTS):
-                nc.tensor.matmul(
-                    windows[a][:].indirect(offsets[:, e * PIECE_COLUMNS : (e + 1) * PIECE_COLUMNS]),
-                    weights[:, e, a * P : (a + 1) * P],
-                    tokens_in[:, e * PIECE : (e + 1) * PIECE],
-                    start=False,
-                    stop=(e == EXPERTS - 1),
-                )
+        in_order_of_loads = [(a, e) for a in range(HALF) for e in range(EXPERTS)]
+        in_order_of_loads += [(a, e) for e in range(EXPERTS) for a in range(HALF, BLOCKS)]
+        for a, e in in_order_of_loads:
+            nc.tensor.matmul(
+                windows[a][:].indirect(offsets[:, e * PIECE_COLUMNS : (e + 1) * PIECE_COLUMNS]),
+                weights[:, e, a * P : (a + 1) * P],
+                tokens_in[:, e * PIECE : (e + 1) * PIECE],
+                start=False,
+                stop=(e == EXPERTS - 1),
+            )
 
         out_blocks = out.rearrange("(a p) t -> a p t", p=P)
         for a in range(BLOCKS):
             result = held.tile([P, TOKENS], F32, name=f"result{a}")
-            nc.vector.tensor_scalar(
-                result[:],
-                windows[a][:],
-                gain_shift[:, a : a + 1],
-                gain_shift[:, BLOCKS + a : BLOCKS + a + 1],
-                op0=mult,
-                op1=add,
-            )
-            nc.sync.dma_start(out_blocks[a], result[:])
+            gain = slice(a, a + 1)
+            shift = slice(BLOCKS + a, BLOCKS + a + 1)
+            if a % 2 == 1:
+                nc.scalar.activation(
+                    result[:],
+                    windows[a][:],
+                    identity_function,
+                    bias=gain_shift_copy[:, shift],
+                    scale=gain_shift_copy[:, gain],
+                )
+                nc.scalar.dma_start(out_blocks[a], result[:])
+            else:
+                shares = 2 if a == 0 else 1
+                for share in range(shares):
+                    columns = slice(share * TOKENS // shares, (share + 1) * TOKENS // shares)
+                    nc.vector.tensor_scalar(
+                        result[:, columns],
+                        windows[a][:, columns],
+                        gain_shift[:, gain],
+                        gain_shift[:, shift],
+                        op0=mult,
+                        op1=add,
+                    )
+                    nc.sync.dma_start(out_blocks[a][:, columns], result[:, columns])

@@ -23,7 +23,6 @@ FLOPS = 2 * P * FEATURES * ENTRIES
 def tile_scatter_matmul_kernel(tc, base, x, w, s, b, offs, out):
     nc = tc.nc
     mult, add = mybir.AluOpType.mult, mybir.AluOpType.add
-    identity_function = mybir.ActivationFunctionType.Identity
 
     with (
         tc.tile_pool(name="held", bufs=1) as held,
@@ -34,9 +33,6 @@ def tile_scatter_matmul_kernel(tc, base, x, w, s, b, offs, out):
         spare_bank = banks.tile([P, WARM_COLUMNS], F32, name="spare_bank")
         for i in range(WARM_MATMULS):
             nc.tensor.matmul(spare_bank[:], zeros[:, 0:P], zeros[:], start=True, stop=True)
-
-        table_warmer = held.tile([P, 1], F32, name="table_warmer")
-        nc.scalar.activation(table_warmer[:], zeros[:, 0:1], identity_function)
 
         HALF = BLOCKS // 2
 
@@ -76,8 +72,6 @@ def tile_scatter_matmul_kernel(tc, base, x, w, s, b, offs, out):
         nc.vector.tensor_copy(ident_f32[:], ident[:])
         gain_shift = banks.tile([P, P], F32, name="gain_shift")
         nc.tensor.transpose(gain_shift[:], gain_shift_rows[:], ident_f32[:])
-        gain_shift_copy = held.tile([P, 2 * BLOCKS], F32, name="gain_shift_copy")
-        nc.vector.tensor_copy(gain_shift_copy[:], gain_shift[:, 0 : 2 * BLOCKS])
 
         in_order_of_loads = [(a, e) for a in range(HALF) for e in range(EXPERTS)]
         in_order_of_loads += [(a, e) for e in range(EXPERTS) for a in range(HALF, BLOCKS)]
@@ -93,27 +87,15 @@ def tile_scatter_matmul_kernel(tc, base, x, w, s, b, offs, out):
         out_blocks = out.rearrange("(a p) t -> a p t", p=P)
         for a in range(BLOCKS):
             result = held.tile([P, TOKENS], F32, name=f"result{a}")
-            gain = slice(a, a + 1)
-            shift = slice(BLOCKS + a, BLOCKS + a + 1)
-            if a % 2 == 1:
-                nc.scalar.activation(
-                    result[:],
-                    windows[a][:],
-                    identity_function,
-                    bias=gain_shift_copy[:, shift],
-                    scale=gain_shift_copy[:, gain],
+            shares = 2 if a == 0 else 1
+            for share in range(shares):
+                columns = slice(share * TOKENS // shares, (share + 1) * TOKENS // shares)
+                nc.vector.tensor_scalar(
+                    result[:, columns],
+                    windows[a][:, columns],
+                    gain_shift[:, a : a + 1],
+                    gain_shift[:, BLOCKS + a : BLOCKS + a + 1],
+                    op0=mult,
+                    op1=add,
                 )
-                nc.scalar.dma_start(out_blocks[a], result[:])
-            else:
-                shares = 2 if a == 0 else 1
-                for share in range(shares):
-                    columns = slice(share * TOKENS // shares, (share + 1) * TOKENS // shares)
-                    nc.vector.tensor_scalar(
-                        result[:, columns],
-                        windows[a][:, columns],
-                        gain_shift[:, gain],
-                        gain_shift[:, shift],
-                        op0=mult,
-                        op1=add,
-                    )
-                    nc.sync.dma_start(out_blocks[a][:, columns], result[:, columns])
+                nc.sync.dma_start(out_blocks[a][:, columns], result[:, columns])

@@ -14,6 +14,8 @@ PIECE = ENTRIES // EXPERTS
 PIECE_COLUMNS = PIECE // 16
 BLOCKS = FEATURES // P
 
+DMA_ALIGN = 256
+
 WARM_COLUMNS = 512
 WARM_MATMULS = 2
 
@@ -40,20 +42,20 @@ def tile_scatter_matmul_kernel(tc, base, x, w, s, b, offs, out):
         nc.sync.dma_start(offsets[:], offs)
 
         base_blocks = base.rearrange("(a p) t -> p a t", p=P)
-        base_rows = held.tile([P, BLOCKS, TOKENS], BF16, name="base_rows")
+        base_rows = held.tile([P, BLOCKS, TOKENS], BF16, name="base_rows", align_bytes=DMA_ALIGN)
         nc.sync.dma_start(base_rows[:, 0:HALF, :], base_blocks[:, 0:HALF, :])
         nc.sync.dma_start(base_rows[:, HALF:BLOCKS, :], base_blocks[:, HALF:BLOCKS, :])
 
-        gain_shift_rows = held.tile([P, P], F32, name="gain_shift_rows")
+        gain_shift_rows = held.tile([P, P], F32, name="gain_shift_rows", align_bytes=DMA_ALIGN)
         nc.gpsimd.memset(gain_shift_rows[:], 0.0)
         nc.sync.dma_start(gain_shift_rows[0:BLOCKS, :], s.rearrange("(a p) o -> a (p o)", p=P))
         nc.sync.dma_start(gain_shift_rows[BLOCKS : 2 * BLOCKS, :], b.rearrange("(a p) o -> a (p o)", p=P))
 
-        tokens_in = held.tile([P, ENTRIES], BF16, name="tokens_in")
+        tokens_in = held.tile([P, ENTRIES], BF16, name="tokens_in", align_bytes=DMA_ALIGN)
         nc.sync.dma_start(tokens_in[:], x)
 
         w_by_k = w.rearrange("e k m -> k e m")
-        weights = held.tile([P, EXPERTS, FEATURES], BF16, name="weights")
+        weights = held.tile([P, EXPERTS, FEATURES], BF16, name="weights", align_bytes=DMA_ALIGN)
         for a in range(HALF):
             columns = slice(a * P, (a + 1) * P)
             nc.sync.dma_start(weights[:, :, columns], w_by_k[:, :, columns])
@@ -86,7 +88,7 @@ def tile_scatter_matmul_kernel(tc, base, x, w, s, b, offs, out):
 
         out_blocks = out.rearrange("(a p) t -> a p t", p=P)
         for a in range(BLOCKS):
-            result = held.tile([P, TOKENS], F32, name=f"result{a}")
+            result = held.tile([P, TOKENS], F32, name=f"result{a}", align_bytes=DMA_ALIGN)
             shares = 2 if a == 0 else 1
             for share in range(shares):
                 columns = slice(share * TOKENS // shares, (share + 1) * TOKENS // shares)

@@ -46,16 +46,16 @@ def tile_scatter_matmul_kernel(tc, base, x, w, s, b, offs, out):
         nc.sync.dma_start(base_rows[:, 0:HALF, :], base_blocks[:, 0:HALF, :])
         nc.sync.dma_start(base_rows[:, HALF:BLOCKS, :], base_blocks[:, HALF:BLOCKS, :])
 
-        gain_shift_rows = held.tile([P, P], F32, name="gain_shift_rows", align_bytes=DMA_ALIGN)
+        gain_shift_rows = held.tile([P, P], F32, name="gain_shift_rows")
         nc.gpsimd.memset(gain_shift_rows[:], 0.0)
         nc.sync.dma_start(gain_shift_rows[0:BLOCKS, :], s.rearrange("(a p) o -> a (p o)", p=P))
         nc.sync.dma_start(gain_shift_rows[BLOCKS : 2 * BLOCKS, :], b.rearrange("(a p) o -> a (p o)", p=P))
 
-        tokens_in = held.tile([P, ENTRIES], BF16, name="tokens_in", align_bytes=DMA_ALIGN)
+        tokens_in = held.tile([P, ENTRIES], BF16, name="tokens_in")
         nc.sync.dma_start(tokens_in[:], x)
 
         w_by_k = w.rearrange("e k m -> k e m")
-        weights = held.tile([P, EXPERTS, FEATURES], BF16, name="weights", align_bytes=DMA_ALIGN)
+        weights = held.tile([P, EXPERTS, FEATURES], BF16, name="weights")
         for a in range(HALF):
             columns = slice(a * P, (a + 1) * P)
             nc.sync.dma_start(weights[:, :, columns], w_by_k[:, :, columns])
@@ -88,7 +88,7 @@ def tile_scatter_matmul_kernel(tc, base, x, w, s, b, offs, out):
 
         out_blocks = out.rearrange("(a p) t -> a p t", p=P)
         for a in range(BLOCKS):
-            result = held.tile([P, TOKENS], F32, name=f"result{a}", align_bytes=DMA_ALIGN)
+            result = held.tile([P, TOKENS], F32, name=f"result{a}")
             shares = 2 if a == 0 else 1
             for share in range(shares):
                 columns = slice(share * TOKENS // shares, (share + 1) * TOKENS // shares)

@@ -43,7 +43,8 @@ def tile_scatter_matmul_kernel(tc, base, x, w, s, b, offs, out):
 
         base_blocks = base.rearrange("(a p) t -> p a t", p=P)
         base_rows = held.tile([P, BLOCKS, TOKENS], BF16, name="base_rows", align_bytes=DMA_ALIGN)
-        nc.sync.dma_start(base_rows[:, 0:HALF, :], base_blocks[:, 0:HALF, :])
+        for a in range(HALF):
+            nc.sync.dma_start(base_rows[:, a, :], base_blocks[:, a, :])
         nc.sync.dma_start(base_rows[:, HALF:BLOCKS, :], base_blocks[:, HALF:BLOCKS, :])
 
         gain_shift_rows = held.tile([P, P], F32, name="gain_shift_rows")

@@ -18,6 +18,7 @@ DMA_ALIGN = 256
 
 WARM_COLUMNS = 512
 WARM_MATMULS = 2
+WARM_EXTRA_COLUMNS = 128
 
 FLOPS = 2 * P * FEATURES * ENTRIES
 
@@ -35,6 +36,9 @@ def tile_scatter_matmul_kernel(tc, base, x, w, s, b, offs, out):
         spare_bank = banks.tile([P, WARM_COLUMNS], F32, name="spare_bank")
         for i in range(WARM_MATMULS):
             nc.tensor.matmul(spare_bank[:], zeros[:, 0:P], zeros[:], start=True, stop=True)
+        nc.tensor.matmul(
+            spare_bank[:, 0:WARM_EXTRA_COLUMNS], zeros[:, 0:P], zeros[:, 0:WARM_EXTRA_COLUMNS], start=True, stop=True
+        )
 
         HALF = BLOCKS // 2
 

import concourse.mybir as mybir
from concourse.masks import make_identity

BF16 = mybir.dt.bfloat16
F32 = mybir.dt.float32
U16 = mybir.dt.uint16

P = 128
TOKENS = 256
FEATURES = 512
ENTRIES = 192
EXPERTS = 2
PIECE = ENTRIES // EXPERTS
PIECE_COLUMNS = PIECE // 16
BLOCKS = FEATURES // P

DMA_ALIGN = 256

WARM_COLUMNS = 512
WARM_MATMULS = 2
WARM_EXTRA_COLUMNS = 128

FLOPS = 2 * P * FEATURES * ENTRIES


def tile_scatter_matmul_kernel(tc, base, x, w, s, b, offs, out):
    nc = tc.nc
    mult, add = mybir.AluOpType.mult, mybir.AluOpType.add

    with (
        tc.tile_pool(name="held", bufs=1) as held,
        tc.psum_pool(name="banks", bufs=1) as banks,
    ):
        zeros = held.tile([P, WARM_COLUMNS], BF16, name="zeros")
        nc.vector.memset(zeros[:], 0.0)
        spare_bank = banks.tile([P, WARM_COLUMNS], F32, name="spare_bank")
        for i in range(WARM_MATMULS):
            nc.tensor.matmul(spare_bank[:], zeros[:, 0:P], zeros[:], start=True, stop=True)
        nc.tensor.matmul(
            spare_bank[:, 0:WARM_EXTRA_COLUMNS], zeros[:, 0:P], zeros[:, 0:WARM_EXTRA_COLUMNS], start=True, stop=True
        )

        HALF = BLOCKS // 2

        offsets = held.tile([P, ENTRIES // 16], U16, name="offsets")
        nc.sync.dma_start(offsets[:], offs)

        base_blocks = base.rearrange("(a p) t -> p a t", p=P)
        base_rows = held.tile([P, BLOCKS, TOKENS], BF16, name="base_rows", align_bytes=DMA_ALIGN)
        for a in range(HALF):
            nc.sync.dma_start(base_rows[:, a, :], base_blocks[:, a, :])
        nc.sync.dma_start(base_rows[:, HALF:BLOCKS, :], base_blocks[:, HALF:BLOCKS, :])

        gain_shift_rows = held.tile([P, P], F32, name="gain_shift_rows")
        nc.gpsimd.memset(gain_shift_rows[:], 0.0)
        nc.sync.dma_start(gain_shift_rows[0:BLOCKS, :], s.rearrange("(a p) o -> a (p o)", p=P))
        nc.sync.dma_start(gain_shift_rows[BLOCKS : 2 * BLOCKS, :], b.rearrange("(a p) o -> a (p o)", p=P))

        tokens_in = held.tile([P, ENTRIES], BF16, name="tokens_in")
        nc.sync.dma_start(tokens_in[:], x)

        w_by_k = w.rearrange("e k m -> k e m")
        weights = held.tile([P, EXPERTS, FEATURES], BF16, name="weights")
        for a in range(HALF):
            columns = slice(a * P, (a + 1) * P)
            nc.sync.dma_start(weights[:, :, columns], w_by_k[:, :, columns])
        last_columns = slice(HALF * P, BLOCKS * P)
        for e in range(EXPERTS):
            nc.sync.dma_start(weights[:, e, last_columns], w_by_k[:, e, last_columns])

        ident = held.tile([P, P], BF16, name="ident")
        make_identity(nc, ident[:])

        windows = [banks.tile([P, TOKENS], F32, name=f"window{a}") for a in range(BLOCKS)]
        for a in range(BLOCKS):
            nc.tensor.matmul(windows[a][:], ident[:], base_rows[:, a, :], start=True, stop=False)

        ident_f32 = held.tile([P, P], F32, name="ident_f32")
        nc.vector.tensor_copy(ident_f32[:], ident[:])
        gain_shift = banks.tile([P, P], F32, name="gain_shift")
        nc.tensor.transpose(gain_shift[:], gain_shift_rows[:], ident_f32[:])

        in_order_of_loads = [(a, e) for a in range(HALF) for e in range(EXPERTS)]
        in_order_of_loads += [(a, e) for e in range(EXPERTS) for a in range(HALF, BLOCKS)]
        for a, e in in_order_of_loads:
            nc.tensor.matmul(
                windows[a][:].indirect(offsets[:, e * PIECE_COLUMNS : (e + 1) * PIECE_COLUMNS]),
                weights[:, e, a * P : (a + 1) * P],
                tokens_in[:, e * PIECE : (e + 1) * PIECE],
                start=False,
                stop=(e == EXPERTS - 1),
            )

        out_blocks = out.rearrange("(a p) t -> a p t", p=P)
        for a in range(BLOCKS):
            result = held.tile([P, TOKENS], F32, name=f"result{a}")
            shares = 2 if a == 0 else 1
            for share in range(shares):
                columns = slice(share * TOKENS // shares, (share + 1) * TOKENS // shares)
                nc.vector.tensor_scalar(
                    result[:, columns],
                    windows[a][:, columns],
                    gain_shift[:, a : a + 1],
                    gain_shift[:, BLOCKS + a : BLOCKS + a + 1],
                    op0=mult,
                    op1=add,
                )
                nc.sync.dma_start(out_blocks[a][:, columns], result[:, columns])
